import numpy as np
import ml_dtypes


def mxq(x, axis, fmt="e4m3"):
    dtype, down = {"e4m3": (ml_dtypes.float8_e4m3fn, 7), "e5m2": (ml_dtypes.float8_e5m2, 14)}[fmt]
    v = np.moveaxis(np.asarray(x, np.float32).astype(ml_dtypes.bfloat16).astype(np.float64), axis, -1)
    blocks = v.reshape(v.shape[:-1] + (-1, 32))
    amax = np.abs(blocks).max(-1, keepdims=True)
    byte = np.maximum(np.where(amax > 0, np.frexp(amax)[1] - 1 + 127, 0) - down, 1)
    scale = np.exp2(byte - 127.0)
    codes = (blocks / scale).astype(np.float32).astype(dtype).astype(np.float64)
    return np.moveaxis((codes * scale).reshape(v.shape), -1, axis)


WIDE = False


def mx_kscale(k):
    if not WIDE:
        return np.ones(k)
    levels = np.array([10, -10, 5, -5, 0])
    if k % 512:
        return np.exp2(np.random.permutation(np.resize(levels, k // 32))).repeat(32)
    a = np.empty((k // 512, 16))
    for p in range(k // 512):
        a[p, :8] = np.random.permutation(np.resize(levels, 8))
        for g in range(8):
            far = levels[np.abs(levels - a[p, g]) >= 10]
            a[p, g + 8] = far[np.random.randint(len(far))]
    return np.exp2(a.ravel()).repeat(32)


def f64(x):
    return np.asarray(x).astype(np.float64)


E2M1 = np.array([0.0, 0.5, 1.0, 1.5, 2.0, 3.0, 4.0, 6.0, -0.0, -0.5, -1.0, -1.5, -2.0, -3.0, -4.0, -6.0])


def pack_weight(w, fmt):
    k, n = w.shape
    w = f64(np.asarray(w, np.float32).astype(ml_dtypes.bfloat16)).reshape(k // 32, 32, n)
    amax = np.abs(w).max(1)
    if fmt == "e4m3":
        byte = np.frexp(amax)[1] - 1 + 127 - 7
    else:
        mant, ex = np.frexp(amax / 6.0)
        byte = np.where(mant > 0.5, ex, ex - 1) + 127
    byte = np.clip(np.where(amax > 0, byte, 1), 1, 254)
    scaled = (w * np.exp2(127.0 - byte)[:, None, :]).reshape(k, n).astype(np.float32)
    by_word = np.ascontiguousarray(scaled.reshape(k // 512, 128, 4, n).transpose(0, 1, 3, 2))
    if fmt == "e4m3":
        words = by_word.astype(ml_dtypes.float8_e4m3fn).view(np.uint8)
    else:
        c = by_word.astype(ml_dtypes.float4_e2m1fn).view(np.uint8) & 0xF
        words = (c[..., 0::2] | (c[..., 1::2] << 4)).reshape(k // 512, 128, 2 * n)
    return np.ascontiguousarray(words), np.ascontiguousarray(byte.astype(np.uint8).reshape(k // 512, 16, n))


def unpack_weight(words, scales, fmt):
    g, _, n = scales.shape
    words = np.ascontiguousarray(words).reshape(g, 128, n, -1)
    if fmt == "e4m3":
        vals = words.view(ml_dtypes.float8_e4m3fn).astype(np.float64)
    else:
        nib = np.empty((g, 128, n, 4), np.uint8)
        nib[..., 0::2] = words & 0xF
        nib[..., 1::2] = words >> 4
        vals = E2M1[nib]
    vals = vals * np.repeat(np.exp2(scales.astype(np.float64) - 127.0), 8, axis=1)[..., None]
    return vals.transpose(0, 1, 3, 2).reshape(g * 512, n)


def planes(y):
    n, m = y.shape
    v = y.astype(np.float32).astype(ml_dtypes.bfloat16).astype(np.float64).reshape(n // 32, 32, m)
    top = np.abs(v).max(1)
    byte = np.clip(np.where(top > 0, np.frexp(top)[1] - 1 + 127 - 7, 1), 1, 254)
    codes = (v * np.exp2(127.0 - byte)[:, None, :]).reshape(n, m).astype(np.float32).astype(ml_dtypes.float8_e4m3fn).view(np.uint8)
    words = codes.reshape(n // 512, 128, 4, m).transpose(0, 1, 3, 2)
    return np.ascontiguousarray(words), np.ascontiguousarray(byte.astype(np.uint8).reshape(n // 512, 16, m))


K, R, M, T = 1024, 512, 1024, 1024


def setup_inputs():
    n = np.random.standard_normal
    s = mx_kscale(K)[:, None]
    u = mx_kscale(R)[:, None]
    p_w4 = pack_weight(n((K, M)) / np.sqrt(K) / s, "e2m1")
    return {
        "x": (n((K, T)) * s).astype(np.float32),
        "w4_words": p_w4[0],
        "w4_scales": p_w4[1],
        "down": (n((K, R)) / np.sqrt(K) / s * u.T).astype(np.float32),
        "up": (0.5 * n((R, M)) / np.sqrt(R) / u).astype(np.float32),
        "g": (n((1024, 1024))).astype(np.float32),
    }


def reference(x, w4_words, w4_scales, down, up, g):
    x_ = mxq(f64(x), 0, "e4m3")
    w4_ = unpack_weight(w4_words, w4_scales, "e2m1")
    down_ = mxq(f64(down), 0, "e4m3")
    up_ = mxq(f64(up), 0, "e4m3")
    h_ = mxq(down_.T @ x_, 0, "e4m3")
    y = x_.T @ w4_ + h_.T @ up_
    out_0 = f64(g) * y
    return (out_0,) + planes(out_0)

from contextlib import ExitStack

import concourse.mybir as mybir

K, R, M, T = 1024, 512, 1024, 1024
FLOPS = 2 * (K * R * T + K * M * T + R * M * T)

F32 = mybir.dt.float32
BF16 = mybir.dt.bfloat16
I32 = mybir.dt.int32
U32 = mybir.dt.uint32
U8 = mybir.dt.uint8
FP8X4 = mybir.dt.float8_e4m3fn_x4
FP4X4 = mybir.dt.float4_e2m1fn_x4
MULT = mybir.AluOpType.mult

P = 128
PACK = 4
KP = P * PACK
NB = 512
DOWN_SPLIT = 3
UP_SPLIT = 80


def tile_mix_lowrank_tm_pl_mul_kernel(tc, x, w4_words, w4_scales, down, up, g, out_0, out_1, out_2):
    nc = tc.nc
    with ExitStack() as ctx:
        sb = ctx.enter_context(tc.tile_pool(name="sb", bufs=1))
        ps = ctx.enter_context(tc.psum_pool(name="ps", bufs=1))
        ctx.enter_context(tc.manual_schedule())

        def tiles(name, count, shape, dtype):
            return [sb.tile(shape, dtype, name="%s%d" % (name, c), align_bytes=64) for c in range(count)]

        x_raw = tiles("x_raw", 2, [P, PACK, T], F32)
        down_raw = tiles("down_raw", 2, [P, PACK, R], F32)
        up_raw = tiles("up_raw", 1, [P, PACK, M], F32)[0]
        g_rows = tiles("g_rows", 2, [P, PACK, M], F32)
        w4_codes = tiles("w4_codes", 1, [P, 2, 2 * M], U8)[0]
        w4_plane = tiles("w4_plane", 1, [P, 2, M], U8)[0]

        x_bf = [tiles("x_bf%d_" % c, 2, [P, PACK * KP], BF16) for c in range(2)]
        x_codes = [tiles("x_codes%d_" % c, 2, [P, KP], U32) for c in range(2)]
        x_plane = [tiles("x_plane%d_" % c, 2, [P, KP], U8) for c in range(2)]
        down_bf = tiles("down_bf", 2, [P, PACK * R], BF16)
        down_codes = tiles("down_codes", 2, [P, R], U32)
        down_plane = tiles("down_plane", 2, [P, R], U8)
        up_bf = tiles("up_bf", 2, [P, PACK * NB], BF16)
        up_codes = tiles("up_codes", 2, [P, NB], U32)
        up_plane = tiles("up_plane", 2, [P, NB], U8)
        h_bf = [tiles("h_bf%d_" % a, 2, [P, PACK * 2 * P], BF16) for a in range(2)]
        h_codes = [tiles("h_codes%d_" % a, 2, [P, 2 * P], U32) for a in range(2)]
        h_plane = [tiles("h_plane%d_" % a, 2, [P, 2 * P], U8) for a in range(2)]
        o_bf = [tiles("o_bf%d_" % a, 2, [P, PACK * NB], BF16) for a in range(2)]
        o_codes = tiles("o_codes", 2, [P, M], U32)
        o_plane = tiles("o_plane", 1, [P, 2, M], U8)[0]

        def bank(b):
            return ps.tile([P, NB], F32, name="bank%d" % b, tag="bank%d" % b)

        def copy(on_vector, dst, src):
            if on_vector:
                nc.vector.tensor_copy(out=dst, in_=src)
            else:
                nc.scalar.copy(out=dst, in_=src)

        def cast_dealt(on_vector, dst, src, i0, i1):
            d = dst[:, i0 * KP : i1 * KP].rearrange("p (i m j) -> p m j i", m=P, j=PACK)
            s = src.rearrange("p j (m i) -> p m j i", i=PACK)
            copy(on_vector, d, s[:, :, :, i0:i1])

        def cast_plain(on_vector, dst, src, c0, c1):
            d = dst.rearrange("p (c e j) -> p c j e", e=PACK, j=PACK)
            s = src.rearrange("p j (c e) -> p c j e", e=PACK)
            copy(on_vector, d[:, c0:c1], s[:, c0:c1])

        def quantize(codes, plane, src):
            nc.vector.quantize_mx(out=codes.bitcast(FP8X4), scales=plane, in_=src)

        def cast_x(c, a):
            cast_dealt(a == 0, x_bf[c][a][:], x_raw[c][:, :, a * KP : (a + 1) * KP], 0, PACK)

        def quantize_x(c, a):
            quantize(x_codes[c][a][:], x_plane[c][a][:], x_bf[c][a][:])

        def h_pass(acc, a, i, c, j):
            cols = slice(i * P, (i + 1) * P)
            rank = slice(j * P, (j + 1) * P)
            nc.tensor.matmul_mx(
                out=acc[:, rank],
                lhsT=down_codes[c][:, rank].bitcast(FP8X4),
                lhsT_scale=down_plane[c][:, rank],
                rhs=x_codes[c][a][:, cols].bitcast(FP8X4),
                rhs_scale=x_plane[c][a][:, cols],
                start=(c == 0 and j == 0),
                stop=(c == 1 and j == PACK - 1),
            )

        def h_out(acc, a, i, on_vector):
            dst = h_bf[a][i // 2][:, (i % 2) * KP : (i % 2 + 1) * KP]
            copy(on_vector, dst.rearrange("p (t j) -> p t j", j=PACK), acc[:].rearrange("p (j t) -> p t j", j=PACK))

        def quantize_h(a, pair):
            quantize(h_codes[a][pair][:], h_plane[a][pair][:], h_bf[a][pair][:])

        def base_pass(acc, a, i, half, c):
            cols = slice(i * P, (i + 1) * P)
            nc.tensor.matmul_mx(
                out=acc[:],
                lhsT=x_codes[c][a][:, cols].bitcast(FP8X4),
                lhsT_scale=x_plane[c][a][:, cols],
                rhs=w4_codes[:, c, 2 * half * NB : 2 * (half + 1) * NB].bitcast(FP4X4),
                rhs_scale=w4_plane[:, c, half * NB : (half + 1) * NB],
                start=(c == 0),
                stop=False,
            )

        def branch_pass(acc, a, i, half):
            cols = slice((i % 2) * P, (i % 2 + 1) * P)
            nc.tensor.matmul_mx(
                out=acc[:],
                lhsT=h_codes[a][i // 2][:, cols].bitcast(FP8X4),
                lhsT_scale=h_plane[a][i // 2][:, cols],
                rhs=up_codes[half][:].bitcast(FP8X4),
                rhs_scale=up_plane[half][:],
                start=False,
                stop=True,
            )

        def multiply(acc, a, i, half):
            rows = g_rows[a][:, i, half * NB : (half + 1) * NB]
            nc.vector.tensor_tensor(out=rows, in0=acc[:], in1=rows, op=MULT)

        def cast_out(on_vector, a, half):
            cast_plain(on_vector, o_bf[a][half][:], g_rows[a][:, :, half * NB : (half + 1) * NB], 0, P)

        def quantize_out(a, half):
            cols = slice(half * NB, (half + 1) * NB)
            quantize(o_codes[a][:, cols], o_plane[:, a, cols], o_bf[a][half][:])

        def pass_rows(t, c):
            return t[c * KP : (c + 1) * KP, :].rearrange("(p j) w -> p j w", j=PACK)

        nc.vector.memset(w4_plane[:].rearrange("p c n -> p (c n)").bitcast(I32), 0)
        for q in range(4):
            nc.scalar.dma_start(
                out=w4_plane[32 * q : 32 * q + 4].bitcast(I32),
                in_=w4_scales[:, 4 * q : 4 * q + 4, :].bitcast(I32).rearrange("c r w -> r c w"),
            )
        nc.sync.dma_start(out=x_raw[0][:], in_=pass_rows(x, 0))
        nc.sync.dma_start(out=down_raw[0][:], in_=pass_rows(down, 0))
        nc.sync.dma_start(out=w4_codes[:].bitcast(I32), in_=w4_words.bitcast(I32).rearrange("c p w -> p c w"))
        nc.sync.dma_start(out=x_raw[1][:], in_=pass_rows(x, 1))
        nc.sync.dma_start(out=down_raw[1][:], in_=pass_rows(down, 1))
        nc.sync.dma_start(out=up_raw[:], in_=pass_rows(up, 0))
        nc.sync.dma_start(out=g_rows[0][:, 0:2, :], in_=pass_rows(g, 0)[:, 0:2, :])
        nc.sync.dma_start(out=g_rows[0][:, 2:4, :], in_=pass_rows(g, 0)[:, 2:4, :])
        nc.sync.dma_start(out=g_rows[1][:], in_=pass_rows(g, 1))

        cast_x(0, 0)
        cast_x(0, 1)
        cast_dealt(False, down_bf[0][:], down_raw[0][:], 0, PACK)
        quantize_x(0, 0)
        quantize_x(0, 1)
        quantize(down_codes[0][:], down_plane[0][:], down_bf[0][:])
        pairs = [[(i, half) for half in range(2) for i in (2 * pair, 2 * pair + 1)] for pair in range(2)]
        h_acc = [bank(i) for i in range(PACK)]
        y_acc = [bank(4 + n) for n in range(4)]
        for i in range(PACK):
            for j in range(PACK):
                h_pass(h_acc[i], 0, i, 0, j)
        for n, (i, half) in enumerate(pairs[0]):
            base_pass(y_acc[n], 0, i, half, 0)

        cast_x(1, 0)
        cast_x(1, 1)
        quantize_x(1, 0)
        for n, (i, half) in enumerate(pairs[0]):
            base_pass(y_acc[n], 0, i, half, 1)
        cast_dealt(True, down_bf[1][:], down_raw[1][:], 0, DOWN_SPLIT)
        cast_dealt(False, down_bf[1][:], down_raw[1][:], DOWN_SPLIT, PACK)
        quantize(down_codes[1][:], down_plane[1][:], down_bf[1][:])
        quantize_x(1, 1)
        for i in range(PACK):
            for j in range(PACK):
                h_pass(h_acc[i], 0, i, 1, j)
        for i in range(PACK):
            h_out(h_acc[i], 0, i, i % 2 == 1)
        quantize_h(0, 0)
        quantize_h(0, 1)

        h_acc = [bank(i) for i in range(PACK)]
        for i in range(PACK):
            for c in range(2):
                for j in range(PACK):
                    h_pass(h_acc[i], 1, i, c, j)
            h_out(h_acc[i], 1, i, False)
        cast_plain(True, up_bf[0][:], up_raw[:, :, 0:NB], 0, P)
        cast_plain(True, up_bf[1][:], up_raw[:, :, NB:M], 0, UP_SPLIT)
        cast_plain(False, up_bf[1][:], up_raw[:, :, NB:M], UP_SPLIT, P)
        quantize(up_codes[0][:], up_plane[0][:], up_bf[0][:])
        quantize(up_codes[1][:], up_plane[1][:], up_bf[1][:])

        y_acc = y_acc + [bank(n) for n in range(4)]
        for n, (i, half) in enumerate(pairs[1]):
            base_pass(y_acc[4 + n], 0, i, half, 0)
            base_pass(y_acc[4 + n], 0, i, half, 1)
        for n, (i, half) in enumerate(pairs[0] + pairs[1]):
            branch_pass(y_acc[n], 0, i, half)
            multiply(y_acc[n], 0, i, half)
            if n == 1:
                quantize_h(1, 0)
            if n == 3:
                quantize_h(1, 1)
        cast_out(False, 0, 0)
        cast_out(False, 0, 1)

        for n, (i, half) in enumerate(pairs[0] + pairs[1]):
            acc = bank((4 + n) % 8)
            base_pass(acc, 1, i, half, 0)
            base_pass(acc, 1, i, half, 1)
            branch_pass(acc, 1, i, half)
            multiply(acc, 1, i, half)
            if n == 4:
                quantize_out(0, 0)
        cast_out(False, 1, 0)
        cast_out(True, 1, 1)
        quantize_out(0, 1)
        quantize_out(1, 1)
        quantize_out(1, 0)

        for a in range(2):
            for pair in range(2):
                rows = slice(2 * pair, 2 * pair + 2)
                nc.sync.dma_start(out=pass_rows(out_0, a)[:, rows, :], in_=g_rows[a][:, rows, :])
        words = out_1.rearrange("a p n i -> a p (n i)").bitcast(I32)
        for a in range(2):
            nc.sync.dma_start(out=words[a], in_=o_codes[a][:].bitcast(I32))
        for q in range(4):
            nc.scalar.dma_start(
                out=out_2[:, 4 * q : 4 * q + 4, :].bitcast(I32).rearrange("a r w -> r a w"),
                in_=o_plane[32 * q : 32 * q + 4].bitcast(I32),
            )
